import numpy as np
import ml_dtypes


def mxq(x, axis, fmt="e4m3"):
    dtype, down = {"e4m3": (ml_dtypes.float8_e4m3fn, 7), "e5m2": (ml_dtypes.float8_e5m2, 14)}[fmt]
    v = np.moveaxis(np.asarray(x, np.float32).astype(ml_dtypes.bfloat16).astype(np.float64), axis, -1)
    blocks = v.reshape(v.shape[:-1] + (-1, 32))
    amax = np.abs(blocks).max(-1, keepdims=True)
    byte = np.maximum(np.where(amax > 0, np.frexp(amax)[1] - 1 + 127, 0) - down, 1)
    scale = np.exp2(byte - 127.0)
    codes = (blocks / scale).astype(np.float32).astype(dtype).astype(np.float64)
    return np.moveaxis((codes * scale).reshape(v.shape), -1, axis)


WIDE = False


def mx_kscale(k):
    if not WIDE:
        return np.ones(k)
    levels = np.array([10, -10, 5, -5, 0])
    if k % 512:
        return np.exp2(np.random.permutation(np.resize(levels, k // 32))).repeat(32)
    a = np.empty((k // 512, 16))
    for p in range(k // 512):
        a[p, :8] = np.random.permutation(np.resize(levels, 8))
        for g in range(8):
            far = levels[np.abs(levels - a[p, g]) >= 10]
            a[p, g + 8] = far[np.random.randint(len(far))]
    return np.exp2(a.ravel()).repeat(32)


def f64(x):
    return np.asarray(x).astype(np.float64)


def striped(idx):
    return np.tile(idx.reshape(-1, 16).T, (8, 1)).astype(np.uint16)


def unstriped(offs):
    return offs[:16].T.reshape(-1).astype(np.int64)


E2M1 = np.array([0.0, 0.5, 1.0, 1.5, 2.0, 3.0, 4.0, 6.0, -0.0, -0.5, -1.0, -1.5, -2.0, -3.0, -4.0, -6.0])


def pack_weight(w, fmt):
    k, n = w.shape
    w = f64(np.asarray(w, np.float32).astype(ml_dtypes.bfloat16)).reshape(k // 32, 32, n)
    amax = np.abs(w).max(1)
    if fmt == "e4m3":
        byte = np.frexp(amax)[1] - 1 + 127 - 7
    else:
        mant, ex = np.frexp(amax / 6.0)
        byte = np.where(mant > 0.5, ex, ex - 1) + 127
    byte = np.clip(np.where(amax > 0, byte, 1), 1, 254)
    scaled = (w * np.exp2(127.0 - byte)[:, None, :]).reshape(k, n).astype(np.float32)
    by_word = np.ascontiguousarray(scaled.reshape(k // 512, 128, 4, n).transpose(0, 1, 3, 2))
    if fmt == "e4m3":
        words = by_word.astype(ml_dtypes.float8_e4m3fn).view(np.uint8)
    else:
        c = by_word.astype(ml_dtypes.float4_e2m1fn).view(np.uint8) & 0xF
        words = (c[..., 0::2] | (c[..., 1::2] << 4)).reshape(k // 512, 128, 2 * n)
    return np.ascontiguousarray(words), np.ascontiguousarray(byte.astype(np.uint8).reshape(k // 512, 16, n))


def unpack_weight(words, scales, fmt):
    g, _, n = scales.shape
    words = np.ascontiguousarray(words).reshape(g, 128, n, -1)
    if fmt == "e4m3":
        vals = words.view(ml_dtypes.float8_e4m3fn).astype(np.float64)
    else:
        nib = np.empty((g, 128, n, 4), np.uint8)
        nib[..., 0::2] = words & 0xF
        nib[..., 1::2] = words >> 4
        vals = E2M1[nib]
    vals = vals * np.repeat(np.exp2(scales.astype(np.float64) - 127.0), 8, axis=1)[..., None]
    return vals.transpose(0, 1, 3, 2).reshape(g * 512, n)


def gelu(v):
    return 0.5 * v * (1.0 + np.tanh(np.sqrt(2.0 / np.pi) * (v + 0.044715 * v**3)))


K, H, T, S, T3, S2, P = 1024, 512, 2048, 1024, 2048, 512, 512

def setup_inputs():
    n = np.random.standard_normal
    s = mx_kscale(K)[:, None]
    u = mx_kscale(H)[:, None]
    tab_words, tab_scales = pack_weight(n((K, T)) * s, "e4m3")
    tab2_words, tab2_scales = pack_weight(n((H, T3)) / np.sqrt(H) / u, "e4m3")
    w2_words, w2_scales = pack_weight(1.4 * n((K, H)) / np.sqrt(K) / s, "e2m1")
    return {
        "tab_words": tab_words, "tab_scales": tab_scales,
        "offs": striped(np.random.permutation(T)[:S]),
        "tab2_words": tab2_words, "tab2_scales": tab2_scales,
        "offs2": striped(np.random.permutation(T3)[:S2]),
        "pos1": striped(np.random.permutation(S)[:P]),
        "pos2": striped(np.random.permutation(S)[:P]),
        "w1": (0.8 * n((K, H)) / np.sqrt(K) / s * u.T).astype(np.float32),
        "b1": (0.4 * n(H) * u[:, 0]).astype(np.float32),
        "w2_words": w2_words, "w2_scales": w2_scales,
        "gain": (np.random.uniform(0.5, 1.5, H) * u[:, 0]).astype(np.float32),
        "w3": (n((H, S2)) / np.sqrt(H) / u).astype(np.float32),
        "calm": np.random.uniform(0.6, 3.0, S2).astype(np.float32),
        "thr": n(S2).astype(np.float32),
        "rubric": n((S2, P)).astype(np.float32),
        "lean": np.random.uniform(0.3, 1.0, S2).astype(np.float32),
    }

def reference(tab_words, tab_scales, offs, tab2_words, tab2_scales, offs2, pos1, pos2,
              w1, b1, w2_words, w2_scales, gain, w3, calm, thr, rubric, lean):
    v = unpack_weight(tab_words, tab_scales, "e4m3")[:, unstriped(offs)]
    v2 = unpack_weight(tab2_words, tab2_scales, "e4m3")[:, unstriped(offs2)]
    w2 = unpack_weight(w2_words, w2_scales, "e2m1")
    h = (mxq(f64(w1), 0, "e4m3").T @ v) + f64(b1)[:, None]
    z = w2.T @ v
    f = f64(gain)[:, None] * (z / (1.0 + np.exp(-z)))
    hq = mxq(h, 0, "e4m3")
    fq = mxq(f, 0, "e4m3")
    e = v2.T @ hq
    d = v2.T @ fq + mxq(f64(w3), 0, "e4m3").T @ hq
    a = 1.0 / (1.0 + np.exp(-(f64(calm)[:, None] * e[:, unstriped(pos1)] + f64(thr)[:, None])))
    return f64(rubric) * a + f64(lean)[:, None] * d[:, unstriped(pos2)]

@@ -1,0 +1,287 @@
+from contextlib import ExitStack
+
+import concourse.mybir as mybir
+
+K, H, T, S, T3, S2, NP = 1024, 512, 2048, 1024, 2048, 512, 512
+FLOPS = 2 * K * H * S * 2 + 2 * H * S2 * S * 3
+
+F32 = mybir.dt.float32
+BF16 = mybir.dt.bfloat16
+I32 = mybir.dt.int32
+U32 = mybir.dt.uint32
+U16 = mybir.dt.uint16
+U8 = mybir.dt.uint8
+FP8X4 = mybir.dt.float8_e4m3fn_x4
+FP4X4 = mybir.dt.float4_e2m1fn_x4
+ALU = mybir.AluOpType
+ACT = mybir.ActivationFunctionType
+
+P = 128
+HALF = 512
+BLK = 128
+
+
+def tile_list_crew_composure_scores_kernel(
+    tc, tab_words, tab_scales, offs, tab2_words, tab2_scales, offs2, pos1, pos2,
+    w1, b1, w2_words, w2_scales, gain, w3, calm, thr, rubric, lean, out,
+):
+    nc = tc.nc
+    with ExitStack() as ctx:
+        keep = ctx.enter_context(tc.tile_pool(name="keep", bufs=1))
+        ring = ctx.enter_context(tc.tile_pool(name="ring", bufs=4))
+        psum = ctx.enter_context(tc.psum_pool(name="psum", bufs=8))
+
+        def kept(name, shape, dtype):
+            return keep.tile(shape, dtype, name=name, align_bytes=64)
+
+        offs_sb = keep.tile([P, S // 16], U16, name="offs_sb")
+        offs2_sb = keep.tile([P, S2 // 16], U16, name="offs2_sb")
+        pos1_sb = keep.tile([P, NP // 16], U16, name="pos1_sb")
+        pos2_sb = keep.tile([P, NP // 16], U16, name="pos2_sb")
+        tab_w = [kept("tab_w%d" % a, [P, T], I32) for a in range(2)]
+        tab_s = kept("tab_s", [P, T // 4], I32)
+        tab2_w = kept("tab2_w", [P, T3], I32)
+        tab2_s = kept("tab2_s", [P, T3 // 4], I32)
+        v_w = [[kept("v_w%d%d" % (a, c), [P, HALF], U32) for c in range(2)] for a in range(2)]
+        v_s = kept("v_s", [P, S], U8)
+        v_s1 = kept("v_s1", [P, S // 4], I32)
+        v2_w = kept("v2_w", [P, S2], U32)
+        v2_s = kept("v2_s", [P, S2], U8)
+        w2_raw = kept("w2_raw", [P, 2 * H // 2], I32)
+        w2s_raw = kept("w2s_raw", [P, 2 * H // 4], I32)
+        w2_w = kept("w2_w", [P, 2 * H], U16)
+        w2_s = kept("w2_s", [P, 2 * H], U8)
+        w1_raw = [kept("w1_raw%d" % a, [P, 4, H], F32) for a in range(2)]
+        w1_b = [kept("w1_b%d" % a, [P, 4 * H], BF16) for a in range(2)]
+        w1_w = [kept("w1_w%d" % a, [P, H], U32) for a in range(2)]
+        w1_s = [kept("w1_s%d" % a, [P, H], U8) for a in range(2)]
+        w3_raw = kept("w3_raw", [P, 4, S2], F32)
+        w3_b = kept("w3_b", [P, 4 * S2], BF16)
+        w3_w = kept("w3_w", [P, S2], U32)
+        w3_s = kept("w3_s", [P, S2], U8)
+        b1_sb = kept("b1_sb", [P, 4], F32)
+        gain_sb = kept("gain_sb", [P, 4], F32)
+        calm_sb = kept("calm_sb", [P, 4], F32)
+        thr_sb = kept("thr_sb", [P, 4], F32)
+        lean_sb = kept("lean_sb", [P, 4], F32)
+        rub_sb = kept("rub_sb", [P, 4, NP], F32)
+        silu_sb = [kept("silu%d" % b, [P, BLK, 4], F32) for b in range(8)]
+        h_b = [kept("h_b%d" % c, [P, 4 * HALF], BF16) for c in range(2)]
+        f_b = [kept("f_b%d" % c, [P, 4 * HALF], BF16) for c in range(2)]
+        h_w = [kept("h_w%d" % c, [P, HALF], U32) for c in range(2)]
+        h_s = [kept("h_s%d" % c, [P, HALF], U8) for c in range(2)]
+        f_w = [kept("f_w%d" % c, [P, HALF], U32) for c in range(2)]
+        f_s = [kept("f_s%d" % c, [P, HALF], U8) for c in range(2)]
+        e_sb = [kept("e_sb%d" % i, [P, S], F32) for i in range(4)]
+        d_sb = [kept("d_sb%d" % i, [P, S], F32) for i in range(4)]
+
+        nc.gpsimd.memset(tab_s[:], 0)
+        nc.vector.memset(v_s1[:], 0)
+        nc.vector.memset(w2s_raw[:], 0)
+        nc.vector.memset(tab2_s[:], 0)
+
+        nc.sync.dma_start(offs_sb[:], offs)
+        for q in range(4):
+            nc.sync.dma_start(out=tab_s[32 * q : 32 * q + 8, :], in_=tab_scales[:, 4 * q : 4 * q + 4, :].bitcast(I32))
+        nc.sync.dma_start(out=tab_w[0][:], in_=tab_words[0].rearrange("p t i -> p (t i)").bitcast(I32))
+        nc.sync.dma_start(offs2_sb[:], offs2)
+        nc.sync.dma_start(
+            out=w2_raw[:].rearrange("p (a c) -> p a c", a=2), in_=w2_words.rearrange("a p c -> p a c").bitcast(I32)
+        )
+        nc.sync.dma_start(out=tab_w[1][:], in_=tab_words[1].rearrange("p t i -> p (t i)").bitcast(I32))
+        for q in range(4):
+            nc.sync.dma_start(
+                out=w2s_raw[32 * q : 32 * q + 4, :].rearrange("r (a c) -> r a c", a=2),
+                in_=w2_scales[:, 4 * q : 4 * q + 4, :].rearrange("a r c -> r a c").bitcast(I32),
+            )
+        nc.sync.dma_start(out=w1_raw[0][:], in_=w1[0:512, :].rearrange("(p j) c -> p j c", j=4))
+        nc.sync.dma_start(out=w1_raw[1][:], in_=w1[512:1024, :].rearrange("(p j) c -> p j c", j=4))
+        nc.sync.dma_start(out=b1_sb[:], in_=b1.rearrange("(p t) -> p t", t=4))
+        nc.sync.dma_start(out=gain_sb[:], in_=gain.rearrange("(p t) -> p t", t=4))
+        for q in range(4):
+            nc.sync.dma_start(out=tab2_s[32 * q : 32 * q + 4, :], in_=tab2_scales[0, 4 * q : 4 * q + 4, :].bitcast(I32))
+        nc.sync.dma_start(out=tab2_w[:], in_=tab2_words[0].rearrange("p t i -> p (t i)").bitcast(I32))
+        nc.sync.dma_start(out=w3_raw[:], in_=w3.rearrange("(p j) c -> p j c", j=4))
+        nc.sync.dma_start(pos1_sb[:], pos1)
+        nc.sync.dma_start(pos2_sb[:], pos2)
+        with nc.allow_non_contiguous_dma(reason="one value a partition"):
+            nc.sync.dma_start(out=calm_sb[:], in_=calm.rearrange("(i p) -> p i", p=P))
+            nc.sync.dma_start(out=thr_sb[:], in_=thr.rearrange("(i p) -> p i", p=P))
+            nc.sync.dma_start(out=lean_sb[:], in_=lean.rearrange("(i p) -> p i", p=P))
+        nc.sync.dma_start(out=rub_sb[:], in_=rubric.rearrange("(i p) n -> p i n", p=P))
+
+        def gather_scales():
+            nc.vector.tensor_copy(v_s[:], tab_s[:].bitcast(U8).indirect(offs_sb[:]))
+            nc.scalar.dma_start(out=v_s1[0:112, :], in_=v_s[4:116, :].bitcast(I32))
+
+        def gather_words(a, c):
+            nc.vector.tensor_copy(v_w[a][c][:], tab_w[a][:].bitcast(U32).indirect(offs_sb[:, 32 * c : 32 * (c + 1)]))
+
+        def v_scale(a, b, from_zero):
+            cols = slice(BLK * b, BLK * (b + 1))
+            if a == 0:
+                return v_s[:, cols]
+            if from_zero:
+                return v_s1[:].bitcast(U8)[:, cols]
+            return v_s[4:P, cols]
+
+        def v_words(a, b):
+            return v_w[a][b // 4][:, BLK * (b % 4) : BLK * (b % 4 + 1)].bitcast(FP8X4)
+
+        def z_block(b):
+            bank = psum.tile([P, 4, BLK], F32, name="bank", tag="bank")
+            w2_bytes = w2_w[:].bitcast(U8)
+            for t in range(4):
+                for a in range(2):
+                    c0 = H * a + P * t
+                    nc.tensor.matmul_mx(
+                        out=bank[:, t, :],
+                        lhsT=w2_bytes[:, 2 * c0 : 2 * (c0 + P)].bitcast(FP4X4), lhsT_scale=w2_s[:, c0 : c0 + P],
+                        rhs=v_words(a, b), rhs_scale=v_scale(a, b, True),
+                        start=(a == 0), stop=(a == 1),
+                    )
+            nc.scalar.activation(out=silu_sb[b][:], in_=bank[:].rearrange("p t j -> p j t"), func=ACT.Silu)
+
+        def f_block(b):
+            dst = f_b[b // 4][:, 512 * (b % 4) : 512 * (b % 4 + 1)].rearrange("p (j t) -> p j t", t=4)
+            nc.vector.tensor_tensor(dst, silu_sb[b][:], gain_sb[:].unsqueeze(1).to_broadcast([P, BLK, 4]), ALU.mult)
+
+        def h_block(b):
+            bank = psum.tile([P, 4, BLK], F32, name="bank", tag="bank")
+            for t in range(4):
+                for a in range(2):
+                    cols = slice(P * t, P * (t + 1))
+                    nc.tensor.matmul_mx(
+                        out=bank[:, t, :],
+                        lhsT=w1_w[a][:, cols].bitcast(FP8X4), lhsT_scale=w1_s[a][:, cols],
+                        rhs=v_words(a, b), rhs_scale=v_scale(a, b, False),
+                        start=(a == 0), stop=(a == 1),
+                    )
+            dst = h_b[b // 4][:, 512 * (b % 4) : 512 * (b % 4 + 1)].rearrange("p (j t) -> p j t", t=4)
+            nc.vector.tensor_tensor(
+                dst, bank[:].rearrange("p t j -> p j t"), b1_sb[:].unsqueeze(1).to_broadcast([P, BLK, 4]), ALU.add
+            )
+
+        def quantize(words, scales, src):
+            nc.vector.quantize_mx(out=words[:].bitcast(FP8X4), scales=scales[:], in_=src[:])
+
+        def w1_views(a):
+            return dict(
+                out=w1_b[a][:].rearrange("p (t m j) -> p m j t", t=4, j=4),
+                in_=w1_raw[a][:].rearrange("p j (m t) -> p m j t", t=4),
+            )
+
+        def weave_w1(a, lo, hi, copy):
+            copy(
+                out=w1_b[a][:].rearrange("p (t m j) -> p m j t", t=4, j=4)[:, lo:hi],
+                in_=w1_raw[a][:].rearrange("p j (m t) -> p m j t", t=4)[:, lo:hi],
+            )
+
+        def e_part(i, c, leave):
+            cols = slice(P * i, P * (i + 1))
+            bank = psum.tile([P, HALF], F32, name="bank", tag="bank")
+            nc.tensor.matmul_mx(
+                out=bank[:], lhsT=v2_w[:, cols].bitcast(FP8X4), lhsT_scale=v2_s[:, cols],
+                rhs=h_w[c][:].bitcast(FP8X4), rhs_scale=h_s[c][:], start=True, stop=True,
+            )
+            leave(out=e_sb[i][:, HALF * c : HALF * (c + 1)], in_=bank[:])
+
+        def d_part(i, c, leave):
+            cols = slice(P * i, P * (i + 1))
+            bank = psum.tile([P, HALF], F32, name="bank", tag="bank")
+            nc.tensor.matmul_mx(
+                out=bank[:], lhsT=w3_w[:, cols].bitcast(FP8X4), lhsT_scale=w3_s[:, cols],
+                rhs=h_w[c][:].bitcast(FP8X4), rhs_scale=h_s[c][:], start=True, stop=False,
+            )
+            nc.tensor.matmul_mx(
+                out=bank[:], lhsT=v2_w[:, cols].bitcast(FP8X4), lhsT_scale=v2_s[:, cols],
+                rhs=f_w[c][:].bitcast(FP8X4), rhs_scale=f_s[c][:], start=False, stop=True,
+            )
+            leave(out=d_sb[i][:, HALF * c : HALF * (c + 1)], in_=bank[:])
+
+        def deal_w2_words():
+            nc.scalar.copy(
+                out=w2_w[:].rearrange("p (a t m) -> p a m t", a=2, t=4),
+                in_=w2_raw[:].bitcast(U16).rearrange("p (a m t) -> p a m t", a=2, t=4),
+            )
+
+        def deal_w2_scales():
+            nc.vector.tensor_copy(
+                out=w2_s[:].rearrange("p (a t m) -> p a m t", a=2, t=4),
+                in_=w2s_raw[:].bitcast(U8).rearrange("p (a m t) -> p a m t", a=2, t=4),
+            )
+
+        def weave_w3(copy):
+            copy(
+                out=w3_b[:].rearrange("p (c i j) -> p c j i", i=4, j=4),
+                in_=w3_raw[:].rearrange("p j (c i) -> p c j i", i=4),
+            )
+
+        seen, weighted, picked = {}, {}, {}
+
+        def look(i):
+            seen[i] = ring.tile([P, NP], F32, name="seen")
+            nc.scalar.activation(
+                out=seen[i][:], in_=e_sb[i][:].indirect(pos1_sb[:]), func=ACT.Sigmoid,
+                bias=thr_sb[:, i : i + 1], scale=calm_sb[:, i : i + 1],
+            )
+
+        def weigh(i, engine):
+            weighted[i] = ring.tile([P, NP], F32, name="weighted")
+            engine.tensor_tensor(weighted[i][:], seen[i][:], rub_sb[:, i, :], ALU.mult)
+
+        def pick(i):
+            picked[i] = ring.tile([P, NP], F32, name="picked")
+            nc.vector.tensor_copy(picked[i][:], d_sb[i][:].indirect(pos2_sb[:]))
+
+        def finish(i):
+            res = ring.tile([P, NP], F32, name="res")
+            nc.vector.scalar_tensor_tensor(
+                res[:], picked[i][:], lean_sb[:, i : i + 1], weighted[i][:], ALU.mult, ALU.add
+            )
+            nc.sync.dma_start(out=out[P * i : P * (i + 1), :], in_=res[:])
+
+        A, V = nc.scalar.copy, nc.vector.tensor_copy
+
+        gather_words(0, 0)
+        gather_scales()
+        gather_words(0, 1)
+        weave_w1(0, 0, 128, A)
+        deal_w2_words()
+        deal_w2_scales()
+        gather_words(1, 0)
+        gather_words(1, 1)
+        weave_w1(1, 0, 128, A)
+        quantize(w1_w[0], w1_s[0], w1_b[0])
+        quantize(w1_w[1], w1_s[1], w1_b[1])
+        for b in range(4):
+            z_block(b)
+        for b in range(4):
+            h_block(b)
+        V(v2_w[:], tab2_w[:].bitcast(U32).indirect(offs2_sb[:]))
+        V(v2_s[:], tab2_s[:].bitcast(U8).indirect(offs2_sb[:]))
+        quantize(h_w[0], h_s[0], h_b[0])
+        for b in range(4, 8):
+            z_block(b)
+        for b in range(4, 8):
+            h_block(b)
+        for i in range(4):
+            e_part(i, 0, A)
+        quantize(h_w[1], h_s[1], h_b[1])
+        for i in range(4):
+            e_part(i, 1, A)
+        weave_w3(A)
+        for b in range(0, 4):
+            f_block(b)
+        quantize(f_w[0], f_s[0], f_b[0])
+        quantize(w3_w, w3_s, w3_b)
+        for b in range(4, 8):
+            f_block(b)
+        quantize(f_w[1], f_s[1], f_b[1])
+        for i in range(4):
+            d_part(i, 0, A)
+            d_part(i, 1, A if i > 1 else V)
+            look(i)
+            pick(i)
+            weigh(i, nc.vector)
+            finish(i)

@@ -29,43 +29,42 @@ def tile_list_crew_composure_scores_kernel(
     with ExitStack() as ctx:
         keep = ctx.enter_context(tc.tile_pool(name="keep", bufs=1))
         ring = ctx.enter_context(tc.tile_pool(name="ring", bufs=4))
-        psum = ctx.enter_context(tc.psum_pool(name="psum", bufs=8))
+        psum = ctx.enter_context(tc.psum_pool(name="psum", bufs=1))
+        banks_taken = []
 
-        def kept(name, shape, dtype):
-            return keep.tile(shape, dtype, name=name, align_bytes=64)
+        def kept(name, shape, dtype, tag=None):
+            return keep.tile(shape, dtype, name=name, tag=tag or name, align_bytes=64)
 
         offs_sb = keep.tile([P, S // 16], U16, name="offs_sb")
         offs2_sb = keep.tile([P, S2 // 16], U16, name="offs2_sb")
         pos1_sb = keep.tile([P, NP // 16], U16, name="pos1_sb")
         pos2_sb = keep.tile([P, NP // 16], U16, name="pos2_sb")
         tab_w = [kept("tab_w%d" % a, [P, T], I32) for a in range(2)]
-        tab_s = kept("tab_s", [P, T // 4], I32)
-        tab2_w = kept("tab2_w", [P, T3], I32)
+        tab_s = kept("tab_s", [P, 2 * T // 4], I32)
         tab2_s = kept("tab2_s", [P, T3 // 4], I32)
-        v_w = [[kept("v_w%d%d" % (a, c), [P, HALF], U32) for c in range(2)] for a in range(2)]
-        v_s = kept("v_s", [P, S], U8)
-        v_s1 = kept("v_s1", [P, S // 4], I32)
+        v_w = [kept("v_w%d" % a, [P, S], U32) for a in range(2)]
+        v_s = [kept("v_s%d" % a, [P, S], U8) for a in range(2)]
         v2_w = kept("v2_w", [P, S2], U32)
         v2_s = kept("v2_s", [P, S2], U8)
         w2_raw = kept("w2_raw", [P, 2 * H // 2], I32)
         w2s_raw = kept("w2s_raw", [P, 2 * H // 4], I32)
         w2_w = kept("w2_w", [P, 2 * H], U16)
         w2_s = kept("w2_s", [P, 2 * H], U8)
-        w1_raw = [kept("w1_raw%d" % a, [P, 4, H], F32) for a in range(2)]
+        w1_raw = [kept("w1_raw%d" % a, [P, 4, H], F32, "stage%d" % a) for a in range(2)]
+        tab2_w = kept("tab2_w", [P, T3], I32, "stage0")
+        w3_raw = kept("w3_raw", [P, 4, S2], F32, "stage1")
+        rub_sb = kept("rub_sb", [P, 4, NP], F32, "stage0")
         w1_b = [kept("w1_b%d" % a, [P, 4 * H], BF16) for a in range(2)]
         w1_w = [kept("w1_w%d" % a, [P, H], U32) for a in range(2)]
         w1_s = [kept("w1_s%d" % a, [P, H], U8) for a in range(2)]
-        w3_raw = kept("w3_raw", [P, 4, S2], F32)
         w3_b = kept("w3_b", [P, 4 * S2], BF16)
         w3_w = kept("w3_w", [P, S2], U32)
         w3_s = kept("w3_s", [P, S2], U8)
         b1_sb = kept("b1_sb", [P, 4], F32)
         gain_sb = kept("gain_sb", [P, 4], F32)
-        calm_sb = kept("calm_sb", [P, 4], F32)
-        thr_sb = kept("thr_sb", [P, 4], F32)
-        lean_sb = kept("lean_sb", [P, 4], F32)
-        rub_sb = kept("rub_sb", [P, 4, NP], F32)
-        silu_sb = [kept("silu%d" % b, [P, BLK, 4], F32) for b in range(8)]
+        rows_sb = kept("rows_sb", [P, 3, 8], F32, "w1_b1")
+        calm_sb, thr_sb, lean_sb = rows_sb[:, 0, 0:4], rows_sb[:, 1, 0:4], rows_sb[:, 2, 0:4]
+        silu_sb = [kept("silu%d" % c, [P, HALF, 4], F32) for c in range(2)]
         h_b = [kept("h_b%d" % c, [P, 4 * HALF], BF16) for c in range(2)]
         f_b = [kept("f_b%d" % c, [P, 4 * HALF], BF16) for c in range(2)]
         h_w = [kept("h_w%d" % c, [P, HALF], U32) for c in range(2)]
@@ -75,61 +74,29 @@ def tile_list_crew_composure_scores_kernel(
         e_sb = [kept("e_sb%d" % i, [P, S], F32) for i in range(4)]
         d_sb = [kept("d_sb%d" % i, [P, S], F32) for i in range(4)]
 
-        nc.gpsimd.memset(tab_s[:], 0)
-        nc.vector.memset(v_s1[:], 0)
+        nc.vector.memset(tab_s[:, 0:512], 0)
+        nc.gpsimd.memset(tab_s[:, 512:1024], 0)
         nc.vector.memset(w2s_raw[:], 0)
         nc.vector.memset(tab2_s[:], 0)
 
-        nc.sync.dma_start(offs_sb[:], offs)
-        for q in range(4):
-            nc.sync.dma_start(out=tab_s[32 * q : 32 * q + 8, :], in_=tab_scales[:, 4 * q : 4 * q + 4, :].bitcast(I32))
-        nc.sync.dma_start(out=tab_w[0][:], in_=tab_words[0].rearrange("p t i -> p (t i)").bitcast(I32))
-        nc.sync.dma_start(offs2_sb[:], offs2)
-        nc.sync.dma_start(
-            out=w2_raw[:].rearrange("p (a c) -> p a c", a=2), in_=w2_words.rearrange("a p c -> p a c").bitcast(I32)
-        )
-        nc.sync.dma_start(out=tab_w[1][:], in_=tab_words[1].rearrange("p t i -> p (t i)").bitcast(I32))
-        for q in range(4):
-            nc.sync.dma_start(
-                out=w2s_raw[32 * q : 32 * q + 4, :].rearrange("r (a c) -> r a c", a=2),
-                in_=w2_scales[:, 4 * q : 4 * q + 4, :].rearrange("a r c -> r a c").bitcast(I32),
-            )
-        nc.sync.dma_start(out=w1_raw[0][:], in_=w1[0:512, :].rearrange("(p j) c -> p j c", j=4))
-        nc.sync.dma_start(out=w1_raw[1][:], in_=w1[512:1024, :].rearrange("(p j) c -> p j c", j=4))
-        nc.sync.dma_start(out=b1_sb[:], in_=b1.rearrange("(p t) -> p t", t=4))
-        nc.sync.dma_start(out=gain_sb[:], in_=gain.rearrange("(p t) -> p t", t=4))
-        for q in range(4):
-            nc.sync.dma_start(out=tab2_s[32 * q : 32 * q + 4, :], in_=tab2_scales[0, 4 * q : 4 * q + 4, :].bitcast(I32))
-        nc.sync.dma_start(out=tab2_w[:], in_=tab2_words[0].rearrange("p t i -> p (t i)").bitcast(I32))
-        nc.sync.dma_start(out=w3_raw[:], in_=w3.rearrange("(p j) c -> p j c", j=4))
-        nc.sync.dma_start(pos1_sb[:], pos1)
-        nc.sync.dma_start(pos2_sb[:], pos2)
-        with nc.allow_non_contiguous_dma(reason="one value a partition"):
-            nc.sync.dma_start(out=calm_sb[:], in_=calm.rearrange("(i p) -> p i", p=P))
-            nc.sync.dma_start(out=thr_sb[:], in_=thr.rearrange("(i p) -> p i", p=P))
-            nc.sync.dma_start(out=lean_sb[:], in_=lean.rearrange("(i p) -> p i", p=P))
-        nc.sync.dma_start(out=rub_sb[:], in_=rubric.rearrange("(i p) n -> p i n", p=P))
+        def gather_scales(a):
+            nc.vector.tensor_copy(v_s[a][:], tab_s[:].bitcast(U8)[:, T * a : T * (a + 1)].indirect(offs_sb[:]))
 
-        def gather_scales():
-            nc.vector.tensor_copy(v_s[:], tab_s[:].bitcast(U8).indirect(offs_sb[:]))
-            nc.scalar.dma_start(out=v_s1[0:112, :], in_=v_s[4:116, :].bitcast(I32))
+        def next_bank(shape):
+            banks_taken.append(len(banks_taken) % 8)
+            return psum.tile(shape, F32, name="bank", tag="bank%d" % banks_taken[-1])
 
-        def gather_words(a, c):
-            nc.vector.tensor_copy(v_w[a][c][:], tab_w[a][:].bitcast(U32).indirect(offs_sb[:, 32 * c : 32 * (c + 1)]))
+        def gather_words(a):
+            nc.vector.tensor_copy(v_w[a][:], tab_w[a][:].bitcast(U32).indirect(offs_sb[:]))
 
-        def v_scale(a, b, from_zero):
-            cols = slice(BLK * b, BLK * (b + 1))
-            if a == 0:
-                return v_s[:, cols]
-            if from_zero:
-                return v_s1[:].bitcast(U8)[:, cols]
-            return v_s[4:P, cols]
+        def v_scale(a, b):
+            return v_s[a][:, BLK * b : BLK * (b + 1)]
 
         def v_words(a, b):
-            return v_w[a][b // 4][:, BLK * (b % 4) : BLK * (b % 4 + 1)].bitcast(FP8X4)
+            return v_w[a][:, BLK * b : BLK * (b + 1)].bitcast(FP8X4)
 
         def z_block(b):
-            bank = psum.tile([P, 4, BLK], F32, name="bank", tag="bank")
+            bank = next_bank([P, 4, BLK])
             w2_bytes = w2_w[:].bitcast(U8)
             for t in range(4):
                 for a in range(2):
@@ -137,24 +104,26 @@ def tile_list_crew_composure_scores_kernel(
                     nc.tensor.matmul_mx(
                         out=bank[:, t, :],
                         lhsT=w2_bytes[:, 2 * c0 : 2 * (c0 + P)].bitcast(FP4X4), lhsT_scale=w2_s[:, c0 : c0 + P],
-                        rhs=v_words(a, b), rhs_scale=v_scale(a, b, True),
+                        rhs=v_words(a, b), rhs_scale=v_scale(a, b),
                         start=(a == 0), stop=(a == 1),
                     )
-            nc.scalar.activation(out=silu_sb[b][:], in_=bank[:].rearrange("p t j -> p j t"), func=ACT.Silu)
+            nc.scalar.activation(out=silu_sb[b // 4][:, BLK * (b % 4) : BLK * (b % 4 + 1), :], in_=bank[:].rearrange("p t j -> p j t"), func=ACT.Silu)
 
-        def f_block(b):
-            dst = f_b[b // 4][:, 512 * (b % 4) : 512 * (b % 4 + 1)].rearrange("p (j t) -> p j t", t=4)
-            nc.vector.tensor_tensor(dst, silu_sb[b][:], gain_sb[:].unsqueeze(1).to_broadcast([P, BLK, 4]), ALU.mult)
+        def f_part(c, lo, hi, engine=nc.vector):
+            dst = f_b[c][:, 4 * lo : 4 * hi].rearrange("p (j t) -> p j t", t=4)
+            engine.tensor_tensor(
+                dst, silu_sb[c][:, lo:hi, :], gain_sb[:].unsqueeze(1).to_broadcast([P, hi - lo, 4]), ALU.mult
+            )
 
         def h_block(b):
-            bank = psum.tile([P, 4, BLK], F32, name="bank", tag="bank")
+            bank = next_bank([P, 4, BLK])
             for t in range(4):
                 for a in range(2):
                     cols = slice(P * t, P * (t + 1))
                     nc.tensor.matmul_mx(
                         out=bank[:, t, :],
                         lhsT=w1_w[a][:, cols].bitcast(FP8X4), lhsT_scale=w1_s[a][:, cols],
-                        rhs=v_words(a, b), rhs_scale=v_scale(a, b, False),
+                        rhs=v_words(a, b), rhs_scale=v_scale(a, b),
                         start=(a == 0), stop=(a == 1),
                     )
             dst = h_b[b // 4][:, 512 * (b % 4) : 512 * (b % 4 + 1)].rearrange("p (j t) -> p j t", t=4)
@@ -179,7 +148,7 @@ def tile_list_crew_composure_scores_kernel(
 
         def e_part(i, c, leave):
             cols = slice(P * i, P * (i + 1))
-            bank = psum.tile([P, HALF], F32, name="bank", tag="bank")
+            bank = next_bank([P, HALF])
             nc.tensor.matmul_mx(
                 out=bank[:], lhsT=v2_w[:, cols].bitcast(FP8X4), lhsT_scale=v2_s[:, cols],
                 rhs=h_w[c][:].bitcast(FP8X4), rhs_scale=h_s[c][:], start=True, stop=True,
@@ -188,7 +157,7 @@ def tile_list_crew_composure_scores_kernel(
 
         def d_part(i, c, leave):
             cols = slice(P * i, P * (i + 1))
-            bank = psum.tile([P, HALF], F32, name="bank", tag="bank")
+            bank = next_bank([P, HALF])
             nc.tensor.matmul_mx(
                 out=bank[:], lhsT=w3_w[:, cols].bitcast(FP8X4), lhsT_scale=w3_s[:, cols],
                 rhs=h_w[c][:].bitcast(FP8X4), rhs_scale=h_s[c][:], start=True, stop=False,
@@ -243,44 +212,76 @@ def tile_list_crew_composure_scores_kernel(
 
         A, V = nc.scalar.copy, nc.vector.tensor_copy
 
-        gather_words(0, 0)
-        gather_scales()
-        gather_words(0, 1)
-        weave_w1(0, 0, 128, A)
+        nc.sync.dma_start(offs_sb[:], offs)
+        nc.sync.dma_start(out=tab_w[0][:], in_=tab_words[0].rearrange("p t i -> p (t i)").bitcast(I32))
+        nc.sync.dma_start(offs2_sb[:], offs2)
+        nc.sync.dma_start(out=tab_w[1][:], in_=tab_words[1].rearrange("p t i -> p (t i)").bitcast(I32))
+        for q in range(4):
+            nc.sync.dma_start(
+                out=tab_s[32 * q : 32 * q + 4, :].rearrange("r (a c) -> r a c", a=2),
+                in_=tab_scales[:, 4 * q : 4 * q + 4, :].rearrange("a r c -> r a c").bitcast(I32),
+            )
+        nc.sync.dma_start(
+            out=w2_raw[:].rearrange("p (a c) -> p a c", a=2), in_=w2_words.rearrange("a p c -> p a c").bitcast(I32)
+        )
+        nc.sync.dma_start(out=w1_raw[0][:], in_=w1[0:512, :].rearrange("(p j) c -> p j c", j=4))
+        nc.sync.dma_start(out=w1_raw[1][:], in_=w1[512:1024, :].rearrange("(p j) c -> p j c", j=4))
+        for q in range(4):
+            nc.sync.dma_start(
+                out=w2s_raw[32 * q : 32 * q + 4, :].rearrange("r (a c) -> r a c", a=2),
+                in_=w2_scales[:, 4 * q : 4 * q + 4, :].rearrange("a r c -> r a c").bitcast(I32),
+            )
+        nc.sync.dma_start(out=b1_sb[:], in_=b1.rearrange("(p t) -> p t", t=4))
+        nc.sync.dma_start(out=gain_sb[:], in_=gain.rearrange("(p t) -> p t", t=4))
+        for q in range(4):
+            nc.sync.dma_start(out=tab2_s[32 * q : 32 * q + 4, :], in_=tab2_scales[0, 4 * q : 4 * q + 4, :].bitcast(I32))
+        nc.sync.dma_start(pos1_sb[:], pos1)
+        nc.sync.dma_start(pos2_sb[:], pos2)
+
+        gather_words(0)
+        gather_words(1)
+        gather_scales(0)
+        gather_scales(1)
         deal_w2_words()
-        deal_w2_scales()
-        gather_words(1, 0)
-        gather_words(1, 1)
+        weave_w1(0, 0, 128, A)
         weave_w1(1, 0, 128, A)
+        nc.sync.dma_start(out=tab2_w[:], in_=tab2_words[0].rearrange("p t i -> p (t i)").bitcast(I32))
+        nc.sync.dma_start(out=w3_raw[:], in_=w3.rearrange("(p j) c -> p j c", j=4))
         quantize(w1_w[0], w1_s[0], w1_b[0])
         quantize(w1_w[1], w1_s[1], w1_b[1])
-        for b in range(4):
-            z_block(b)
+        deal_w2_scales()
+        with nc.allow_non_contiguous_dma(reason="one value a partition"):
+            nc.sync.dma_start(out=calm_sb, in_=calm.rearrange("(i p) -> p i", p=P))
+            nc.sync.dma_start(out=thr_sb, in_=thr.rearrange("(i p) -> p i", p=P))
+            nc.sync.dma_start(out=lean_sb, in_=lean.rearrange("(i p) -> p i", p=P))
+        weave_w3(A)
         for b in range(4):
             h_block(b)
-        V(v2_w[:], tab2_w[:].bitcast(U32).indirect(offs2_sb[:]))
-        V(v2_s[:], tab2_s[:].bitcast(U8).indirect(offs2_sb[:]))
         quantize(h_w[0], h_s[0], h_b[0])
-        for b in range(4, 8):
+        V(v2_s[:], tab2_s[:].bitcast(U8).indirect(offs2_sb[:]))
+        V(v2_w[:], tab2_w[:].bitcast(U32).indirect(offs2_sb[:]))
+        nc.sync.dma_start(out=rub_sb[:], in_=rubric.rearrange("(i p) n -> p i n", p=P))
+        for b in range(4):
             z_block(b)
         for b in range(4, 8):
             h_block(b)
+        quantize(h_w[1], h_s[1], h_b[1])
+        for b in range(4, 8):
+            z_block(b)
         for i in range(4):
             e_part(i, 0, A)
-        quantize(h_w[1], h_s[1], h_b[1])
         for i in range(4):
             e_part(i, 1, A)
-        weave_w3(A)
-        for b in range(0, 4):
-            f_block(b)
+        for lo in range(0, HALF, 512):
+            f_part(0, lo, lo + 512)
         quantize(f_w[0], f_s[0], f_b[0])
         quantize(w3_w, w3_s, w3_b)
-        for b in range(4, 8):
-            f_block(b)
+        for lo in range(0, HALF, 512):
+            f_part(1, lo, lo + 512)
         quantize(f_w[1], f_s[1], f_b[1])
         for i in range(4):
-            d_part(i, 0, A)
-            d_part(i, 1, A if i > 1 else V)
+            for c in range(2):
+                d_part(i, c, V if 2 * i + c < 3 else A)
             look(i)
             pick(i)
             weigh(i, nc.vector)

@@ -3,7 +3,7 @@ from contextlib import ExitStack
 import concourse.mybir as mybir
 
 K, H, T, S, T3, S2, NP = 1024, 512, 2048, 1024, 2048, 512, 512
-FLOPS = 2 * K * H * S * 2 + 2 * H * S2 * S * 3
+FLOPS = 2 * (2 * K * H * S) + 3 * (2 * H * S2 * S)
 
 F32 = mybir.dt.float32
 BF16 = mybir.dt.bfloat16
@@ -17,8 +17,20 @@ ALU = mybir.AluOpType
 ACT = mybir.ActivationFunctionType
 
 P = 128
-HALF = 512
-BLK = 128
+PACK = 4
+K_PASS = P * PACK
+PASSES = K // K_PASS
+QUADRANTS = 4
+BANKS = 8
+BANK_COLS = 512
+BLOCK = BANK_COLS // PACK
+HALF = BANK_COLS
+HALVES = S // HALF
+BLOCKS_IN_HALF = HALF // BLOCK
+ROW_TILES = S2 // P
+LIST_ROWS = 16
+ROW_VECTOR_PAD = 8
+D_TILES_ON_VECTOR = 2
 
 
 def tile_list_crew_composure_scores_kernel(
@@ -28,261 +40,231 @@ def tile_list_crew_composure_scores_kernel(
     nc = tc.nc
     with ExitStack() as ctx:
         keep = ctx.enter_context(tc.tile_pool(name="keep", bufs=1))
-        ring = ctx.enter_context(tc.tile_pool(name="ring", bufs=4))
+        ring = ctx.enter_context(tc.tile_pool(name="ring", bufs=ROW_TILES))
         psum = ctx.enter_context(tc.psum_pool(name="psum", bufs=1))
+
+        def kept(name, shape, dtype, reuses=None):
+            return keep.tile(shape, dtype, name=name, tag=reuses or name, align_bytes=64)
+
         banks_taken = []
 
-        def kept(name, shape, dtype, tag=None):
-            return keep.tile(shape, dtype, name=name, tag=tag or name, align_bytes=64)
-
-        offs_sb = keep.tile([P, S // 16], U16, name="offs_sb")
-        offs2_sb = keep.tile([P, S2 // 16], U16, name="offs2_sb")
-        pos1_sb = keep.tile([P, NP // 16], U16, name="pos1_sb")
-        pos2_sb = keep.tile([P, NP // 16], U16, name="pos2_sb")
-        tab_w = [kept("tab_w%d" % a, [P, T], I32) for a in range(2)]
-        tab_s = kept("tab_s", [P, 2 * T // 4], I32)
-        tab2_s = kept("tab2_s", [P, T3 // 4], I32)
-        v_w = [kept("v_w%d" % a, [P, S], U32) for a in range(2)]
-        v_s = [kept("v_s%d" % a, [P, S], U8) for a in range(2)]
-        v2_w = kept("v2_w", [P, S2], U32)
-        v2_s = kept("v2_s", [P, S2], U8)
-        w2_raw = kept("w2_raw", [P, 2 * H // 2], I32)
-        w2s_raw = kept("w2s_raw", [P, 2 * H // 4], I32)
-        w2_w = kept("w2_w", [P, 2 * H], U16)
-        w2_s = kept("w2_s", [P, 2 * H], U8)
-        w1_raw = [kept("w1_raw%d" % a, [P, 4, H], F32, "stage%d" % a) for a in range(2)]
-        tab2_w = kept("tab2_w", [P, T3], I32, "stage0")
-        w3_raw = kept("w3_raw", [P, 4, S2], F32, "stage1")
-        rub_sb = kept("rub_sb", [P, 4, NP], F32, "stage0")
-        w1_b = [kept("w1_b%d" % a, [P, 4 * H], BF16) for a in range(2)]
-        w1_w = [kept("w1_w%d" % a, [P, H], U32) for a in range(2)]
-        w1_s = [kept("w1_s%d" % a, [P, H], U8) for a in range(2)]
-        w3_b = kept("w3_b", [P, 4 * S2], BF16)
-        w3_w = kept("w3_w", [P, S2], U32)
-        w3_s = kept("w3_s", [P, S2], U8)
-        b1_sb = kept("b1_sb", [P, 4], F32)
-        gain_sb = kept("gain_sb", [P, 4], F32)
-        rows_sb = kept("rows_sb", [P, 3, 8], F32, "w1_b1")
-        calm_sb, thr_sb, lean_sb = rows_sb[:, 0, 0:4], rows_sb[:, 1, 0:4], rows_sb[:, 2, 0:4]
-        silu_sb = [kept("silu%d" % c, [P, HALF, 4], F32) for c in range(2)]
-        h_b = [kept("h_b%d" % c, [P, 4 * HALF], BF16) for c in range(2)]
-        f_b = [kept("f_b%d" % c, [P, 4 * HALF], BF16) for c in range(2)]
-        h_w = [kept("h_w%d" % c, [P, HALF], U32) for c in range(2)]
-        h_s = [kept("h_s%d" % c, [P, HALF], U8) for c in range(2)]
-        f_w = [kept("f_w%d" % c, [P, HALF], U32) for c in range(2)]
-        f_s = [kept("f_s%d" % c, [P, HALF], U8) for c in range(2)]
-        e_sb = [kept("e_sb%d" % i, [P, S], F32) for i in range(4)]
-        d_sb = [kept("d_sb%d" % i, [P, S], F32) for i in range(4)]
-
-        nc.vector.memset(tab_s[:, 0:512], 0)
-        nc.gpsimd.memset(tab_s[:, 512:1024], 0)
-        nc.vector.memset(w2s_raw[:], 0)
-        nc.vector.memset(tab2_s[:], 0)
-
-        def gather_scales(a):
-            nc.vector.tensor_copy(v_s[a][:], tab_s[:].bitcast(U8)[:, T * a : T * (a + 1)].indirect(offs_sb[:]))
-
         def next_bank(shape):
-            banks_taken.append(len(banks_taken) % 8)
+            banks_taken.append(len(banks_taken) % BANKS)
             return psum.tile(shape, F32, name="bank", tag="bank%d" % banks_taken[-1])
 
-        def gather_words(a):
-            nc.vector.tensor_copy(v_w[a][:], tab_w[a][:].bitcast(U32).indirect(offs_sb[:]))
+        offs_sb = keep.tile([P, S // LIST_ROWS], U16, name="offs_sb")
+        offs2_sb = keep.tile([P, S2 // LIST_ROWS], U16, name="offs2_sb")
+        pos1_sb = keep.tile([P, NP // LIST_ROWS], U16, name="pos1_sb")
+        pos2_sb = keep.tile([P, NP // LIST_ROWS], U16, name="pos2_sb")
+        tab_w = [kept("tab_w%d" % a, [P, T], I32) for a in range(PASSES)]
+        tab_s = kept("tab_s", [P, PASSES * T // 4], I32)
+        tab2_s = kept("tab2_s", [P, T3 // 4], I32)
+        v_w = [kept("v_w%d" % a, [P, S], U32) for a in range(PASSES)]
+        v_s = [[kept("v_s%d%d" % (a, c), [P, HALF], U8) for c in range(HALVES)] for a in range(PASSES)]
+        v2_w = kept("v2_w", [P, S2], U32)
+        v2_s = kept("v2_s", [P, S2], U8)
+        w2_raw = kept("w2_raw", [P, PASSES * H // 2], I32)
+        w2s_raw = kept("w2s_raw", [P, PASSES * H // 4], I32)
+        w2_w = kept("w2_w", [P, PASSES * H], U16)
+        w2_s = kept("w2_s", [P, PASSES * H], U8)
+        w1_raw = [kept("w1_raw%d" % a, [P, PACK, H], F32) for a in range(PASSES)]
+        tab2_w = kept("tab2_w", [P, T3], I32, reuses="w1_raw0")
+        w3_raw = kept("w3_raw", [P, PACK, S2], F32)
+        rub_sb = kept("rub_sb", [P, ROW_TILES, NP], F32, reuses="w1_raw0")
+        w1_b = [kept("w1_b%d" % a, [P, PACK * H], BF16) for a in range(PASSES)]
+        w1_w = [kept("w1_w%d" % a, [P, H], U32) for a in range(PASSES)]
+        w1_s = [kept("w1_s%d" % a, [P, H], U8) for a in range(PASSES)]
+        w3_b = kept("w3_b", [P, PACK * S2], BF16)
+        w3_w = kept("w3_w", [P, S2], U32)
+        w3_s = kept("w3_s", [P, S2], U8)
+        b1_sb = kept("b1_sb", [P, PACK], F32)
+        gain_sb = kept("gain_sb", [P, PACK], F32)
+        row_vectors = kept("row_vectors", [P, 3, ROW_VECTOR_PAD], F32, reuses="w1_b0")
+        calm_sb, thr_sb, lean_sb = [row_vectors[:, n, 0:ROW_TILES] for n in range(3)]
+        silu_sb = [kept("silu%d" % c, [P, HALF, PACK], F32) for c in range(HALVES)]
+        h_b = [kept("h_b%d" % c, [P, PACK * HALF], BF16) for c in range(HALVES)]
+        f_b = [kept("f_b0", [P, PACK * HALF], BF16, reuses="w1_b1"), kept("f_b1", [P, PACK * HALF], BF16)]
+        h_w = [kept("h_w%d" % c, [P, HALF], U32) for c in range(HALVES)]
+        h_s = [kept("h_s%d" % c, [P, HALF], U8) for c in range(HALVES)]
+        f_w = [kept("f_w%d" % c, [P, HALF], U32) for c in range(HALVES)]
+        f_s = [kept("f_s%d" % c, [P, HALF], U8) for c in range(HALVES)]
+        e_sb = [kept("e_sb%d" % i, [P, S], F32) for i in range(ROW_TILES)]
+        d_sb = [kept("d_sb%d" % i, [P, S], F32) for i in range(ROW_TILES)]
 
-        def v_scale(a, b):
-            return v_s[a][:, BLK * b : BLK * (b + 1)]
+        def load_words(tile, words):
+            nc.sync.dma_start(out=tile[:], in_=words.rearrange("p t i -> p (t i)").bitcast(I32))
 
-        def v_words(a, b):
-            return v_w[a][:, BLK * b : BLK * (b + 1)].bitcast(FP8X4)
+        def load_scale_rows(tile, scales):
+            for quad in range(QUADRANTS):
+                nc.sync.dma_start(
+                    out=tile[32 * quad : 32 * quad + 4, :].rearrange("r (a c) -> r a c", a=scales.shape[0]),
+                    in_=scales[:, 4 * quad : 4 * quad + 4, :].rearrange("a r c -> r a c").bitcast(I32),
+                )
 
-        def z_block(b):
-            bank = next_bank([P, 4, BLK])
-            w2_bytes = w2_w[:].bitcast(U8)
-            for t in range(4):
-                for a in range(2):
-                    c0 = H * a + P * t
+        def load_pass(tile, rows):
+            nc.sync.dma_start(out=tile[:], in_=rows.rearrange("(p j) c -> p j c", j=PACK))
+
+        def gather_words(dst, table, offsets):
+            nc.vector.tensor_copy(dst[:], table[:].bitcast(U32).indirect(offsets[:]))
+
+        def gather_tab_scales(c):
+            entries = offs_sb[:, HALF // LIST_ROWS * c : HALF // LIST_ROWS * (c + 1)]
+            for a in range(PASSES):
+                nc.vector.tensor_copy(v_s[a][c][:], tab_s[:].bitcast(U8)[:, T * a : T * (a + 1)].indirect(entries))
+
+        def quantize(words, scales, woven):
+            nc.vector.quantize_mx(out=words[:].bitcast(FP8X4), scales=scales[:], in_=woven[:])
+
+        def first_stage_bank(b, weight):
+            bank = next_bank([P, PACK, BLOCK])
+            c, lo = divmod(BLOCK * b, HALF)
+            for t in range(PACK):
+                for a in range(PASSES):
+                    codes, scales = weight(a, t)
                     nc.tensor.matmul_mx(
-                        out=bank[:, t, :],
-                        lhsT=w2_bytes[:, 2 * c0 : 2 * (c0 + P)].bitcast(FP4X4), lhsT_scale=w2_s[:, c0 : c0 + P],
-                        rhs=v_words(a, b), rhs_scale=v_scale(a, b),
-                        start=(a == 0), stop=(a == 1),
+                        out=bank[:, t, :], lhsT=codes, lhsT_scale=scales,
+                        rhs=v_w[a][:, BLOCK * b : BLOCK * (b + 1)].bitcast(FP8X4),
+                        rhs_scale=v_s[a][c][:, lo : lo + BLOCK],
+                        start=(a == 0), stop=(a == PASSES - 1),
                     )
-            nc.scalar.activation(out=silu_sb[b // 4][:, BLK * (b % 4) : BLK * (b % 4 + 1), :], in_=bank[:].rearrange("p t j -> p j t"), func=ACT.Silu)
+            return bank[:].rearrange("p t j -> p j t"), c, lo
 
-        def f_part(c, lo, hi, engine=nc.vector):
-            dst = f_b[c][:, 4 * lo : 4 * hi].rearrange("p (j t) -> p j t", t=4)
-            engine.tensor_tensor(
-                dst, silu_sb[c][:, lo:hi, :], gain_sb[:].unsqueeze(1).to_broadcast([P, hi - lo, 4]), ALU.mult
-            )
+        def w1_slice(a, t):
+            return w1_w[a][:, P * t : P * (t + 1)].bitcast(FP8X4), w1_s[a][:, P * t : P * (t + 1)]
+
+        def w2_slice(a, t):
+            first = H * a + P * t
+            return w2_w[:].bitcast(U8)[:, 2 * first : 2 * (first + P)].bitcast(FP4X4), w2_s[:, first : first + P]
+
+        def woven_columns(tile, lo, hi):
+            return tile[:, PACK * lo : PACK * hi].rearrange("p (j t) -> p j t", t=PACK)
+
+        def per_row(vector, columns):
+            return vector[:].unsqueeze(1).to_broadcast([P, columns, PACK])
+
+        def silu_block(b):
+            sums, c, lo = first_stage_bank(b, w2_slice)
+            nc.scalar.activation(out=silu_sb[c][:, lo : lo + BLOCK, :], in_=sums, func=ACT.Silu)
 
         def h_block(b):
-            bank = next_bank([P, 4, BLK])
-            for t in range(4):
-                for a in range(2):
-                    cols = slice(P * t, P * (t + 1))
-                    nc.tensor.matmul_mx(
-                        out=bank[:, t, :],
-                        lhsT=w1_w[a][:, cols].bitcast(FP8X4), lhsT_scale=w1_s[a][:, cols],
-                        rhs=v_words(a, b), rhs_scale=v_scale(a, b),
-                        start=(a == 0), stop=(a == 1),
-                    )
-            dst = h_b[b // 4][:, 512 * (b % 4) : 512 * (b % 4 + 1)].rearrange("p (j t) -> p j t", t=4)
-            nc.vector.tensor_tensor(
-                dst, bank[:].rearrange("p t j -> p j t"), b1_sb[:].unsqueeze(1).to_broadcast([P, BLK, 4]), ALU.add
+            sums, c, lo = first_stage_bank(b, w1_slice)
+            nc.vector.tensor_tensor(woven_columns(h_b[c], lo, lo + BLOCK), sums, per_row(b1_sb, BLOCK), ALU.add)
+
+        def f_columns(engine, c, lo, hi):
+            engine.tensor_tensor(
+                woven_columns(f_b[c], lo, hi), silu_sb[c][:, lo:hi, :], per_row(gain_sb, hi - lo), ALU.mult
             )
 
-        def quantize(words, scales, src):
-            nc.vector.quantize_mx(out=words[:].bitcast(FP8X4), scales=scales[:], in_=src[:])
-
-        def w1_views(a):
-            return dict(
-                out=w1_b[a][:].rearrange("p (t m j) -> p m j t", t=4, j=4),
-                in_=w1_raw[a][:].rearrange("p j (m t) -> p m j t", t=4),
-            )
-
-        def weave_w1(a, lo, hi, copy):
-            copy(
-                out=w1_b[a][:].rearrange("p (t m j) -> p m j t", t=4, j=4)[:, lo:hi],
-                in_=w1_raw[a][:].rearrange("p j (m t) -> p m j t", t=4)[:, lo:hi],
-            )
-
-        def e_part(i, c, leave):
-            cols = slice(P * i, P * (i + 1))
+        def scores(dst, i, c, products, copy):
+            rows = slice(P * i, P * (i + 1))
             bank = next_bank([P, HALF])
-            nc.tensor.matmul_mx(
-                out=bank[:], lhsT=v2_w[:, cols].bitcast(FP8X4), lhsT_scale=v2_s[:, cols],
-                rhs=h_w[c][:].bitcast(FP8X4), rhs_scale=h_s[c][:], start=True, stop=True,
-            )
-            leave(out=e_sb[i][:, HALF * c : HALF * (c + 1)], in_=bank[:])
+            for n, (lhs_w, lhs_s, rhs_w, rhs_s) in enumerate(products):
+                nc.tensor.matmul_mx(
+                    out=bank[:], lhsT=lhs_w[:, rows].bitcast(FP8X4), lhsT_scale=lhs_s[:, rows],
+                    rhs=rhs_w[:].bitcast(FP8X4), rhs_scale=rhs_s[:],
+                    start=(n == 0), stop=(n == len(products) - 1),
+                )
+            copy(out=dst[i][:, HALF * c : HALF * (c + 1)], in_=bank[:])
 
-        def d_part(i, c, leave):
-            cols = slice(P * i, P * (i + 1))
-            bank = next_bank([P, HALF])
-            nc.tensor.matmul_mx(
-                out=bank[:], lhsT=w3_w[:, cols].bitcast(FP8X4), lhsT_scale=w3_s[:, cols],
-                rhs=h_w[c][:].bitcast(FP8X4), rhs_scale=h_s[c][:], start=True, stop=False,
-            )
-            nc.tensor.matmul_mx(
-                out=bank[:], lhsT=v2_w[:, cols].bitcast(FP8X4), lhsT_scale=v2_s[:, cols],
-                rhs=f_w[c][:].bitcast(FP8X4), rhs_scale=f_s[c][:], start=False, stop=True,
-            )
-            leave(out=d_sb[i][:, HALF * c : HALF * (c + 1)], in_=bank[:])
-
-        def deal_w2_words():
-            nc.scalar.copy(
-                out=w2_w[:].rearrange("p (a t m) -> p a m t", a=2, t=4),
-                in_=w2_raw[:].bitcast(U16).rearrange("p (a m t) -> p a m t", a=2, t=4),
-            )
-
-        def deal_w2_scales():
-            nc.vector.tensor_copy(
-                out=w2_s[:].rearrange("p (a t m) -> p a m t", a=2, t=4),
-                in_=w2s_raw[:].bitcast(U8).rearrange("p (a m t) -> p a m t", a=2, t=4),
-            )
-
-        def weave_w3(copy):
-            copy(
-                out=w3_b[:].rearrange("p (c i j) -> p c j i", i=4, j=4),
-                in_=w3_raw[:].rearrange("p j (c i) -> p c j i", i=4),
-            )
-
-        seen, weighted, picked = {}, {}, {}
-
-        def look(i):
-            seen[i] = ring.tile([P, NP], F32, name="seen")
-            nc.scalar.activation(
-                out=seen[i][:], in_=e_sb[i][:].indirect(pos1_sb[:]), func=ACT.Sigmoid,
-                bias=thr_sb[:, i : i + 1], scale=calm_sb[:, i : i + 1],
-            )
-
-        def weigh(i, engine):
-            weighted[i] = ring.tile([P, NP], F32, name="weighted")
-            engine.tensor_tensor(weighted[i][:], seen[i][:], rub_sb[:, i, :], ALU.mult)
-
-        def pick(i):
-            picked[i] = ring.tile([P, NP], F32, name="picked")
-            nc.vector.tensor_copy(picked[i][:], d_sb[i][:].indirect(pos2_sb[:]))
-
-        def finish(i):
-            res = ring.tile([P, NP], F32, name="res")
-            nc.vector.scalar_tensor_tensor(
-                res[:], picked[i][:], lean_sb[:, i : i + 1], weighted[i][:], ALU.mult, ALU.add
-            )
-            nc.sync.dma_start(out=out[P * i : P * (i + 1), :], in_=res[:])
-
-        A, V = nc.scalar.copy, nc.vector.tensor_copy
+        nc.vector.memset(tab_s[:, 0 : T // 4], 0)
+        nc.gpsimd.memset(w2s_raw[:], 0)
+        nc.gpsimd.memset(tab_s[:, T // 4 :], 0)
+        nc.vector.memset(tab2_s[:], 0)
 
         nc.sync.dma_start(offs_sb[:], offs)
-        nc.sync.dma_start(out=tab_w[0][:], in_=tab_words[0].rearrange("p t i -> p (t i)").bitcast(I32))
+        load_words(tab_w[0], tab_words[0])
         nc.sync.dma_start(offs2_sb[:], offs2)
-        nc.sync.dma_start(out=tab_w[1][:], in_=tab_words[1].rearrange("p t i -> p (t i)").bitcast(I32))
-        for q in range(4):
-            nc.sync.dma_start(
-                out=tab_s[32 * q : 32 * q + 4, :].rearrange("r (a c) -> r a c", a=2),
-                in_=tab_scales[:, 4 * q : 4 * q + 4, :].rearrange("a r c -> r a c").bitcast(I32),
-            )
-        nc.sync.dma_start(
-            out=w2_raw[:].rearrange("p (a c) -> p a c", a=2), in_=w2_words.rearrange("a p c -> p a c").bitcast(I32)
-        )
-        nc.sync.dma_start(out=w1_raw[0][:], in_=w1[0:512, :].rearrange("(p j) c -> p j c", j=4))
-        nc.sync.dma_start(out=w1_raw[1][:], in_=w1[512:1024, :].rearrange("(p j) c -> p j c", j=4))
-        for q in range(4):
-            nc.sync.dma_start(
-                out=w2s_raw[32 * q : 32 * q + 4, :].rearrange("r (a c) -> r a c", a=2),
-                in_=w2_scales[:, 4 * q : 4 * q + 4, :].rearrange("a r c -> r a c").bitcast(I32),
-            )
-        nc.sync.dma_start(out=b1_sb[:], in_=b1.rearrange("(p t) -> p t", t=4))
-        nc.sync.dma_start(out=gain_sb[:], in_=gain.rearrange("(p t) -> p t", t=4))
-        for q in range(4):
-            nc.sync.dma_start(out=tab2_s[32 * q : 32 * q + 4, :], in_=tab2_scales[0, 4 * q : 4 * q + 4, :].bitcast(I32))
         nc.sync.dma_start(pos1_sb[:], pos1)
+        load_scale_rows(w2s_raw, w2_scales)
+        load_words(tab_w[1], tab_words[1])
+        load_scale_rows(tab_s, tab_scales)
+        nc.sync.dma_start(
+            out=w2_raw[:].rearrange("p (a c) -> p a c", a=PASSES),
+            in_=w2_words.rearrange("a p c -> p a c").bitcast(I32),
+        )
+        for a in range(PASSES):
+            load_pass(w1_raw[a], w1[K_PASS * a : K_PASS * (a + 1), :])
+        load_pass(w3_raw, w3)
+        nc.sync.dma_start(out=b1_sb[:], in_=b1.rearrange("(p t) -> p t", t=PACK))
+        nc.sync.dma_start(out=gain_sb[:], in_=gain.rearrange("(p t) -> p t", t=PACK))
+        for quad in range(QUADRANTS):
+            nc.sync.dma_start(
+                out=tab2_s[32 * quad : 32 * quad + 4, :], in_=tab2_scales[0, 4 * quad : 4 * quad + 4, :].bitcast(I32)
+            )
         nc.sync.dma_start(pos2_sb[:], pos2)
 
-        gather_words(0)
-        gather_words(1)
-        gather_scales(0)
-        gather_scales(1)
-        deal_w2_words()
-        weave_w1(0, 0, 128, A)
-        weave_w1(1, 0, 128, A)
-        nc.sync.dma_start(out=tab2_w[:], in_=tab2_words[0].rearrange("p t i -> p (t i)").bitcast(I32))
-        nc.sync.dma_start(out=w3_raw[:], in_=w3.rearrange("(p j) c -> p j c", j=4))
-        quantize(w1_w[0], w1_s[0], w1_b[0])
-        quantize(w1_w[1], w1_s[1], w1_b[1])
-        deal_w2_scales()
-        with nc.allow_non_contiguous_dma(reason="one value a partition"):
-            nc.sync.dma_start(out=calm_sb, in_=calm.rearrange("(i p) -> p i", p=P))
-            nc.sync.dma_start(out=thr_sb, in_=thr.rearrange("(i p) -> p i", p=P))
-            nc.sync.dma_start(out=lean_sb, in_=lean.rearrange("(i p) -> p i", p=P))
-        weave_w3(A)
-        for b in range(4):
+        for a in range(PASSES):
+            gather_words(v_w[a], tab_w[a], offs_sb)
+        gather_tab_scales(0)
+        nc.gpsimd.tensor_copy(
+            out=w2_s[:].rearrange("p (a t m) -> p a t m", a=PASSES, t=PACK),
+            in_=w2s_raw[:].bitcast(U8).rearrange("p (a m t) -> p a t m", a=PASSES, t=PACK),
+        )
+        gather_tab_scales(1)
+        nc.scalar.copy(
+            out=w2_w[:].rearrange("p (a t m) -> p a m t", a=PASSES, t=PACK),
+            in_=w2_raw[:].bitcast(U16).rearrange("p (a m t) -> p a m t", a=PASSES, t=PACK),
+        )
+        for a in range(PASSES):
+            nc.scalar.copy(
+                out=w1_b[a][:].rearrange("p (t m j) -> p m j t", t=PACK, j=PACK),
+                in_=w1_raw[a][:].rearrange("p j (m t) -> p m j t", t=PACK),
+            )
+        load_words(tab2_w, tab2_words[0])
+        for a in range(PASSES):
+            quantize(w1_w[a], w1_s[a], w1_b[a])
+        with nc.allow_non_contiguous_dma(reason="one value a partition for each row tile"):
+            for tile, vector in ((calm_sb, calm), (thr_sb, thr), (lean_sb, lean)):
+                nc.sync.dma_start(out=tile, in_=vector.rearrange("(i p) -> p i", p=P))
+
+        for b in range(BLOCKS_IN_HALF):
+            silu_block(b)
+        for b in range(HALVES * BLOCKS_IN_HALF):
             h_block(b)
         quantize(h_w[0], h_s[0], h_b[0])
-        V(v2_s[:], tab2_s[:].bitcast(U8).indirect(offs2_sb[:]))
-        V(v2_w[:], tab2_w[:].bitcast(U32).indirect(offs2_sb[:]))
+        nc.vector.tensor_copy(v2_s[:], tab2_s[:].bitcast(U8).indirect(offs2_sb[:]))
+        gather_words(v2_w, tab2_w, offs2_sb)
         nc.sync.dma_start(out=rub_sb[:], in_=rubric.rearrange("(i p) n -> p i n", p=P))
-        for b in range(4):
-            z_block(b)
-        for b in range(4, 8):
-            h_block(b)
         quantize(h_w[1], h_s[1], h_b[1])
-        for b in range(4, 8):
-            z_block(b)
-        for i in range(4):
-            e_part(i, 0, A)
-        for i in range(4):
-            e_part(i, 1, A)
-        for lo in range(0, HALF, 512):
-            f_part(0, lo, lo + 512)
+        for b in range(BLOCKS_IN_HALF, HALVES * BLOCKS_IN_HALF):
+            silu_block(b)
+        nc.scalar.copy(
+            out=w3_b[:].rearrange("p (g i j) -> p g j i", i=4, j=PACK),
+            in_=w3_raw[:].rearrange("p j (g i) -> p g j i", i=4),
+        )
+
+        for c in range(HALVES):
+            for i in range(ROW_TILES):
+                scores(e_sb, i, c, [(v2_w, v2_s, h_w[c], h_s[c])], nc.scalar.copy)
+
+        for lo in range(0, HALF, BLOCK):
+            f_columns(nc.gpsimd, 0, lo, lo + BLOCK)
         quantize(f_w[0], f_s[0], f_b[0])
         quantize(w3_w, w3_s, w3_b)
-        for lo in range(0, HALF, 512):
-            f_part(1, lo, lo + 512)
+        f_columns(nc.vector, 1, 0, HALF)
         quantize(f_w[1], f_s[1], f_b[1])
-        for i in range(4):
-            for c in range(2):
-                d_part(i, c, V if 2 * i + c < 3 else A)
-            look(i)
-            pick(i)
-            weigh(i, nc.vector)
-            finish(i)
+
+        for i in range(ROW_TILES):
+            copy = nc.vector.tensor_copy if i < D_TILES_ON_VECTOR else nc.scalar.copy
+            for c in range(HALVES):
+                scores(d_sb, i, c, [(w3_w, w3_s, h_w[c], h_s[c]), (v2_w, v2_s, f_w[c], f_s[c])], copy)
+            width = NP if i < ROW_TILES - 1 else NP // 2
+            pieces = [slice(lo, lo + width) for lo in range(0, NP, width)]
+            seen = ring.tile([P, NP], F32, name="seen")
+            for cols in pieces:
+                entries = pos1_sb[:, cols.start // LIST_ROWS : cols.stop // LIST_ROWS]
+                nc.scalar.activation(
+                    out=seen[:, cols], in_=e_sb[i][:].indirect(entries), func=ACT.Sigmoid,
+                    bias=thr_sb[:, i : i + 1], scale=calm_sb[:, i : i + 1],
+                )
+            picked = ring.tile([P, NP], F32, name="picked")
+            nc.vector.tensor_copy(picked[:], d_sb[i][:].indirect(pos2_sb[:]))
+            weighted = ring.tile([P, NP], F32, name="weighted")
+            for cols in pieces:
+                nc.vector.tensor_tensor(weighted[:, cols], seen[:, cols], rub_sb[:, i, cols], ALU.mult)
+            result = ring.tile([P, NP], F32, name="result")
+            for cols in pieces:
+                nc.vector.scalar_tensor_tensor(
+                    result[:, cols], picked[:, cols], lean_sb[:, i : i + 1], weighted[:, cols], ALU.mult, ALU.add
+                )
+                nc.sync.dma_start(out=out[P * i : P * (i + 1), cols], in_=result[:, cols])

from contextlib import ExitStack

import concourse.mybir as mybir

K, H, T, S, T3, S2, NP = 1024, 512, 2048, 1024, 2048, 512, 512
FLOPS = 2 * (2 * K * H * S) + 3 * (2 * H * S2 * S)

F32 = mybir.dt.float32
BF16 = mybir.dt.bfloat16
I32 = mybir.dt.int32
U32 = mybir.dt.uint32
U16 = mybir.dt.uint16
U8 = mybir.dt.uint8
FP8X4 = mybir.dt.float8_e4m3fn_x4
FP4X4 = mybir.dt.float4_e2m1fn_x4
ALU = mybir.AluOpType
ACT = mybir.ActivationFunctionType

P = 128
PACK = 4
K_PASS = P * PACK
PASSES = K // K_PASS
QUADRANTS = 4
BANKS = 8
BANK_COLS = 512
BLOCK = BANK_COLS // PACK
HALF = BANK_COLS
HALVES = S // HALF
BLOCKS_IN_HALF = HALF // BLOCK
ROW_TILES = S2 // P
LIST_ROWS = 16
ROW_VECTOR_PAD = 8
D_TILES_ON_VECTOR = 2


def tile_list_crew_composure_scores_kernel(
    tc, tab_words, tab_scales, offs, tab2_words, tab2_scales, offs2, pos1, pos2,
    w1, b1, w2_words, w2_scales, gain, w3, calm, thr, rubric, lean, out,
):
    nc = tc.nc
    with ExitStack() as ctx:
        keep = ctx.enter_context(tc.tile_pool(name="keep", bufs=1))
        ring = ctx.enter_context(tc.tile_pool(name="ring", bufs=ROW_TILES))
        psum = ctx.enter_context(tc.psum_pool(name="psum", bufs=1))

        def kept(name, shape, dtype, reuses=None):
            return keep.tile(shape, dtype, name=name, tag=reuses or name, align_bytes=64)

        banks_taken = []

        def next_bank(shape):
            banks_taken.append(len(banks_taken) % BANKS)
            return psum.tile(shape, F32, name="bank", tag="bank%d" % banks_taken[-1])

        offs_sb = keep.tile([P, S // LIST_ROWS], U16, name="offs_sb")
        offs2_sb = keep.tile([P, S2 // LIST_ROWS], U16, name="offs2_sb")
        pos1_sb = keep.tile([P, NP // LIST_ROWS], U16, name="pos1_sb")
        pos2_sb = keep.tile([P, NP // LIST_ROWS], U16, name="pos2_sb")
        tab_w = [kept("tab_w%d" % a, [P, T], I32) for a in range(PASSES)]
        tab_s = kept("tab_s", [P, PASSES * T // 4], I32)
        tab2_s = kept("tab2_s", [P, T3 // 4], I32)
        v_w = [kept("v_w%d" % a, [P, S], U32) for a in range(PASSES)]
        v_s = [[kept("v_s%d%d" % (a, c), [P, HALF], U8) for c in range(HALVES)] for a in range(PASSES)]
        v2_w = kept("v2_w", [P, S2], U32)
        v2_s = kept("v2_s", [P, S2], U8)
        w2_raw = kept("w2_raw", [P, PASSES * H // 2], I32)
        w2s_raw = kept("w2s_raw", [P, PASSES * H // 4], I32)
        w2_w = kept("w2_w", [P, PASSES * H], U16)
        w2_s = kept("w2_s", [P, PASSES * H], U8)
        w1_raw = [kept("w1_raw%d" % a, [P, PACK, H], F32) for a in range(PASSES)]
        tab2_w = kept("tab2_w", [P, T3], I32, reuses="w1_raw0")
        w3_raw = kept("w3_raw", [P, PACK, S2], F32)
        rub_sb = kept("rub_sb", [P, ROW_TILES, NP], F32, reuses="w1_raw0")
        w1_b = [kept("w1_b%d" % a, [P, PACK * H], BF16) for a in range(PASSES)]
        w1_w = [kept("w1_w%d" % a, [P, H], U32) for a in range(PASSES)]
        w1_s = [kept("w1_s%d" % a, [P, H], U8) for a in range(PASSES)]
        w3_b = kept("w3_b", [P, PACK * S2], BF16)
        w3_w = kept("w3_w", [P, S2], U32)
        w3_s = kept("w3_s", [P, S2], U8)
        b1_sb = kept("b1_sb", [P, PACK], F32)
        gain_sb = kept("gain_sb", [P, PACK], F32)
        row_vectors = kept("row_vectors", [P, 3, ROW_VECTOR_PAD], F32, reuses="w1_b0")
        calm_sb, thr_sb, lean_sb = [row_vectors[:, n, 0:ROW_TILES] for n in range(3)]
        silu_sb = [kept("silu%d" % c, [P, HALF, PACK], F32) for c in range(HALVES)]
        h_b = [kept("h_b%d" % c, [P, PACK * HALF], BF16) for c in range(HALVES)]
        f_b = [kept("f_b0", [P, PACK * HALF], BF16, reuses="w1_b1"), kept("f_b1", [P, PACK * HALF], BF16)]
        h_w = [kept("h_w%d" % c, [P, HALF], U32) for c in range(HALVES)]
        h_s = [kept("h_s%d" % c, [P, HALF], U8) for c in range(HALVES)]
        f_w = [kept("f_w%d" % c, [P, HALF], U32) for c in range(HALVES)]
        f_s = [kept("f_s%d" % c, [P, HALF], U8) for c in range(HALVES)]
        e_sb = [kept("e_sb%d" % i, [P, S], F32) for i in range(ROW_TILES)]
        d_sb = [kept("d_sb%d" % i, [P, S], F32) for i in range(ROW_TILES)]

        def load_words(tile, words):
            nc.sync.dma_start(out=tile[:], in_=words.rearrange("p t i -> p (t i)").bitcast(I32))

        def load_scale_rows(tile, scales):
            for quad in range(QUADRANTS):
                nc.sync.dma_start(
                    out=tile[32 * quad : 32 * quad + 4, :].rearrange("r (a c) -> r a c", a=scales.shape[0]),
                    in_=scales[:, 4 * quad : 4 * quad + 4, :].rearrange("a r c -> r a c").bitcast(I32),
                )

        def load_pass(tile, rows):
            nc.sync.dma_start(out=tile[:], in_=rows.rearrange("(p j) c -> p j c", j=PACK))

        def gather_words(dst, table, offsets):
            nc.vector.tensor_copy(dst[:], table[:].bitcast(U32).indirect(offsets[:]))

        def gather_tab_scales(c):
            entries = offs_sb[:, HALF // LIST_ROWS * c : HALF // LIST_ROWS * (c + 1)]
            for a in range(PASSES):
                nc.vector.tensor_copy(v_s[a][c][:], tab_s[:].bitcast(U8)[:, T * a : T * (a + 1)].indirect(entries))

        def quantize(words, scales, woven):
            nc.vector.quantize_mx(out=words[:].bitcast(FP8X4), scales=scales[:], in_=woven[:])

        def first_stage_bank(b, weight):
            bank = next_bank([P, PACK, BLOCK])
            c, lo = divmod(BLOCK * b, HALF)
            for t in range(PACK):
                for a in range(PASSES):
                    codes, scales = weight(a, t)
                    nc.tensor.matmul_mx(
                        out=bank[:, t, :], lhsT=codes, lhsT_scale=scales,
                        rhs=v_w[a][:, BLOCK * b : BLOCK * (b + 1)].bitcast(FP8X4),
                        rhs_scale=v_s[a][c][:, lo : lo + BLOCK],
                        start=(a == 0), stop=(a == PASSES - 1),
                    )
            return bank[:].rearrange("p t j -> p j t"), c, lo

        def w1_slice(a, t):
            return w1_w[a][:, P * t : P * (t + 1)].bitcast(FP8X4), w1_s[a][:, P * t : P * (t + 1)]

        def w2_slice(a, t):
            first = H * a + P * t
            return w2_w[:].bitcast(U8)[:, 2 * first : 2 * (first + P)].bitcast(FP4X4), w2_s[:, first : first + P]

        def woven_columns(tile, lo, hi):
            return tile[:, PACK * lo : PACK * hi].rearrange("p (j t) -> p j t", t=PACK)

        def per_row(vector, columns):
            return vector[:].unsqueeze(1).to_broadcast([P, columns, PACK])

        def silu_block(b):
            sums, c, lo = first_stage_bank(b, w2_slice)
            nc.scalar.activation(out=silu_sb[c][:, lo : lo + BLOCK, :], in_=sums, func=ACT.Silu)

        def h_block(b):
            sums, c, lo = first_stage_bank(b, w1_slice)
            nc.vector.tensor_tensor(woven_columns(h_b[c], lo, lo + BLOCK), sums, per_row(b1_sb, BLOCK), ALU.add)

        def f_columns(engine, c, lo, hi):
            engine.tensor_tensor(
                woven_columns(f_b[c], lo, hi), silu_sb[c][:, lo:hi, :], per_row(gain_sb, hi - lo), ALU.mult
            )

        def scores(dst, i, c, products, copy):
            rows = slice(P * i, P * (i + 1))
            bank = next_bank([P, HALF])
            for n, (lhs_w, lhs_s, rhs_w, rhs_s) in enumerate(products):
                nc.tensor.matmul_mx(
                    out=bank[:], lhsT=lhs_w[:, rows].bitcast(FP8X4), lhsT_scale=lhs_s[:, rows],
                    rhs=rhs_w[:].bitcast(FP8X4), rhs_scale=rhs_s[:],
                    start=(n == 0), stop=(n == len(products) - 1),
                )
            copy(out=dst[i][:, HALF * c : HALF * (c + 1)], in_=bank[:])

        nc.vector.memset(tab_s[:, 0 : T // 4], 0)
        nc.gpsimd.memset(w2s_raw[:], 0)
        nc.gpsimd.memset(tab_s[:, T // 4 :], 0)
        nc.vector.memset(tab2_s[:], 0)

        nc.sync.dma_start(offs_sb[:], offs)
        load_words(tab_w[0], tab_words[0])
        nc.sync.dma_start(offs2_sb[:], offs2)
        nc.sync.dma_start(pos1_sb[:], pos1)
        load_scale_rows(w2s_raw, w2_scales)
        load_words(tab_w[1], tab_words[1])
        load_scale_rows(tab_s, tab_scales)
        nc.sync.dma_start(
            out=w2_raw[:].rearrange("p (a c) -> p a c", a=PASSES),
            in_=w2_words.rearrange("a p c -> p a c").bitcast(I32),
        )
        for a in range(PASSES):
            load_pass(w1_raw[a], w1[K_PASS * a : K_PASS * (a + 1), :])
        load_pass(w3_raw, w3)
        nc.sync.dma_start(out=b1_sb[:], in_=b1.rearrange("(p t) -> p t", t=PACK))
        nc.sync.dma_start(out=gain_sb[:], in_=gain.rearrange("(p t) -> p t", t=PACK))
        for quad in range(QUADRANTS):
            nc.sync.dma_start(
                out=tab2_s[32 * quad : 32 * quad + 4, :], in_=tab2_scales[0, 4 * quad : 4 * quad + 4, :].bitcast(I32)
            )
        nc.sync.dma_start(pos2_sb[:], pos2)

        for a in range(PASSES):
            gather_words(v_w[a], tab_w[a], offs_sb)
        gather_tab_scales(0)
        nc.gpsimd.tensor_copy(
            out=w2_s[:].rearrange("p (a t m) -> p a t m", a=PASSES, t=PACK),
            in_=w2s_raw[:].bitcast(U8).rearrange("p (a m t) -> p a t m", a=PASSES, t=PACK),
        )
        gather_tab_scales(1)
        nc.scalar.copy(
            out=w2_w[:].rearrange("p (a t m) -> p a m t", a=PASSES, t=PACK),
            in_=w2_raw[:].bitcast(U16).rearrange("p (a m t) -> p a m t", a=PASSES, t=PACK),
        )
        for a in range(PASSES):
            nc.scalar.copy(
                out=w1_b[a][:].rearrange("p (t m j) -> p m j t", t=PACK, j=PACK),
                in_=w1_raw[a][:].rearrange("p j (m t) -> p m j t", t=PACK),
            )
        load_words(tab2_w, tab2_words[0])
        for a in range(PASSES):
            quantize(w1_w[a], w1_s[a], w1_b[a])
        with nc.allow_non_contiguous_dma(reason="one value a partition for each row tile"):
            for tile, vector in ((calm_sb, calm), (thr_sb, thr), (lean_sb, lean)):
                nc.sync.dma_start(out=tile, in_=vector.rearrange("(i p) -> p i", p=P))

        for b in range(BLOCKS_IN_HALF):
            silu_block(b)
        for b in range(HALVES * BLOCKS_IN_HALF):
            h_block(b)
        quantize(h_w[0], h_s[0], h_b[0])
        nc.vector.tensor_copy(v2_s[:], tab2_s[:].bitcast(U8).indirect(offs2_sb[:]))
        gather_words(v2_w, tab2_w, offs2_sb)
        nc.sync.dma_start(out=rub_sb[:], in_=rubric.rearrange("(i p) n -> p i n", p=P))
        quantize(h_w[1], h_s[1], h_b[1])
        for b in range(BLOCKS_IN_HALF, HALVES * BLOCKS_IN_HALF):
            silu_block(b)
        nc.scalar.copy(
            out=w3_b[:].rearrange("p (g i j) -> p g j i", i=4, j=PACK),
            in_=w3_raw[:].rearrange("p j (g i) -> p g j i", i=4),
        )

        for c in range(HALVES):
            for i in range(ROW_TILES):
                scores(e_sb, i, c, [(v2_w, v2_s, h_w[c], h_s[c])], nc.scalar.copy)

        for lo in range(0, HALF, BLOCK):
            f_columns(nc.gpsimd, 0, lo, lo + BLOCK)
        quantize(f_w[0], f_s[0], f_b[0])
        quantize(w3_w, w3_s, w3_b)
        f_columns(nc.vector, 1, 0, HALF)
        quantize(f_w[1], f_s[1], f_b[1])

        for i in range(ROW_TILES):
            copy = nc.vector.tensor_copy if i < D_TILES_ON_VECTOR else nc.scalar.copy
            for c in range(HALVES):
                scores(d_sb, i, c, [(w3_w, w3_s, h_w[c], h_s[c]), (v2_w, v2_s, f_w[c], f_s[c])], copy)
            width = NP if i < ROW_TILES - 1 else NP // 2
            pieces = [slice(lo, lo + width) for lo in range(0, NP, width)]
            seen = ring.tile([P, NP], F32, name="seen")
            for cols in pieces:
                entries = pos1_sb[:, cols.start // LIST_ROWS : cols.stop // LIST_ROWS]
                nc.scalar.activation(
                    out=seen[:, cols], in_=e_sb[i][:].indirect(entries), func=ACT.Sigmoid,
                    bias=thr_sb[:, i : i + 1], scale=calm_sb[:, i : i + 1],
                )
            picked = ring.tile([P, NP], F32, name="picked")
            nc.vector.tensor_copy(picked[:], d_sb[i][:].indirect(pos2_sb[:]))
            weighted = ring.tile([P, NP], F32, name="weighted")
            for cols in pieces:
                nc.vector.tensor_tensor(weighted[:, cols], seen[:, cols], rub_sb[:, i, cols], ALU.mult)
            result = ring.tile([P, NP], F32, name="result")
            for cols in pieces:
                nc.vector.scalar_tensor_tensor(
                    result[:, cols], picked[:, cols], lean_sb[:, i : i + 1], weighted[:, cols], ALU.mult, ALU.add
                )
                nc.sync.dma_start(out=out[P * i : P * (i + 1), cols], in_=result[:, cols])
